import numpy as np, ml_dtypes
CORES = [5,29,101,125,133,157,229,253]
N = 8
import mx_ref
BF = ml_dtypes.bfloat16
def gentries(a):
    return np.ascontiguousarray(a.reshape(8, 16, -1).transpose(0, 2, 1)).reshape(8, -1)
def gtable(e):
    e = np.asarray(e); return np.ascontiguousarray(e.reshape(8, -1, 16).transpose(0, 2, 1)).reshape(128, -1).astype(np.int32)
def gcols(t, e):
    v = np.concatenate([t.reshape(8, 16, -1, 4), np.zeros((8, 16, 1, 4), BF)], axis=2)
    return np.ascontiguousarray(np.stack([v[g][:, e[g]] for g in range(8)])).reshape(128, -1)
def gpick(z, e):
    return np.concatenate([z[16 * g:16 * g + 16][:, e[g]] for g in range(8)])
def tile(rs):
    return np.stack(rs, axis=2).reshape(128, -1).astype(BF)
def pick(q, e):
    c = np.concatenate([q[0].reshape(128, -1, 4), np.zeros((128, 1, 4), np.uint8)], axis=1); s = np.concatenate([q[1], np.ones((16, 1), np.uint8)], axis=1)
    return (np.ascontiguousarray(c[:, e].reshape(128, -1)), np.ascontiguousarray(s[:, e]))
def join(*qs):
    return (np.concatenate([q[0] for q in qs], axis=1), np.concatenate([q[1] for q in qs], axis=1))
def put(q, e, v):
    c, s = q[0].reshape(128, -1, 4).copy(), q[1].copy(); c[:, e] = v[0].reshape(128, -1, 4); s[:, e] = v[1]
    return (c.reshape(128, -1), s)
def pk(c, s):
    return (np.ascontiguousarray(c), mx_ref.live(s))
def emit(q):
    return q[0], q[1]
def packed(v, rng):
    q = [mx_ref.quantize(np.ascontiguousarray(v[r])) for r in range(N)]
    return np.stack([a for a, b in q]), np.stack([mx_ref.plane(b, rng) for a, b in q])
def values_of_codes():
    e, c = np.zeros((128, 128, 4), np.float32), np.zeros((128, 2, 4), np.uint8)
    e[np.arange(128), np.arange(128), 0] = 1
    c[:127, :, 0] = np.arange(256).reshape(2, 128).T[:127]
    return mx_ref.matmul(mx_ref.quantize(e.reshape(128, 512).astype(BF)), (c.reshape(128, 8), np.full((16, 2), 127, np.uint8))).T.reshape(-1).astype(np.float64)
CODE_VALUE, SCALE_VALUE = values_of_codes(), 2.0 ** (np.arange(256) - 127.0)
def decode(q):
    return (CODE_VALUE[q[0]].reshape(16, 8, -1, 4) * SCALE_VALUE[q[1]][:, None, :, None] + 0.0).reshape(128, -1).astype(np.float32)
def f(rng, *shape):
    return mx_ref.flush((rng.standard_normal(shape, dtype=np.float32) * np.exp2(rng.integers(-2, 3, shape[:-1] + (1,)))).astype(BF))
def wide(rng, *shape, cols=0):
    v = rng.standard_normal(shape, dtype=np.float32) * np.exp2(rng.integers(-12, 13, shape)).astype(np.float32)
    if cols: v *= np.repeat(np.exp2(rng.integers(-cols, cols + 1, shape[:-2] + (1, shape[-1] // 4))) * (rng.random(shape[:-2] + (1, shape[-1] // 4)) > 0.0625), 4, axis=-1).astype(np.float32)
    return mx_ref.flush(v.astype(BF))
C, H = 288, 144
STEP = [4, 1, 2]
G, OWN = np.arange(8)[:, None], np.tile(np.arange(C), (8, 1))
def numbers_of(rng):
    return {"x": np.array(f(rng, N, 128, 4 * C)), "u": np.array(f(rng, N, 128, 512)), "v": np.array(f(rng, N, 128, 512))}
def stored(a, m):
    return {"fl": np.stack([gtable(a[r]) for r in range(N)]), "ml": np.stack([gtable(m[r]) for r in range(N)])}
def pairs(o):
    m = np.zeros(o.shape, np.int64)
    np.put_along_axis(m, o[..., ::2], o[..., 1::2], axis=-1)
    np.put_along_axis(m, o[..., 1::2], o[..., ::2], axis=-1)
    return m
def ring(o):
    a = np.zeros(C, np.int64)
    a[o] = np.roll(o, -1)
    return a
def lists(rng):
    e = np.tile(np.arange(C), (N, 8, 1))
    return rng.permuted(e, axis=2), pairs(rng.permuted(e, axis=2))
def layers(rng, still=[]):
    w = np.array(f(rng, N, 128, 2048)).reshape(N, 8, 16, 4, 8, 16, 4)
    for i in still:
        w[:, :, i] = 0
        w[:, :, :, :, :, i] = 0
    return w
def weights(rng, w):
    c, s = packed(np.ascontiguousarray(w).reshape(N, 128, 2048), rng)
    return {"wc": c, "ws": s}
def parity():
    i = np.arange(N)
    return (i ^ (i >> 1) ^ (i >> 2)) % 2
def setup_inputs(rng):
    return {**numbers_of(rng), **stored(*lists(rng)), **weights(rng, layers(rng))}
def setup_inputs_ties(rng):
    d = numbers_of(rng)
    o = rng.permutation(N)
    k = rng.integers(0, 4, (N, 8, C))
    k[o[1]] += 1
    k[o[2], rng.permutation(8)[:4]] = 1
    a, m = lists(rng)
    g = int(rng.integers(8))
    a[:, g] = np.arange(C)
    m[:, g] = (np.arange(C) + H) % C
    k[o[3], g] = np.arange(C) >= H
    x = d["x"].reshape(N, 8, 16, C, 4)
    x[:, :, 0] = 0
    x[:, :, 0, :, 0] = k.astype(np.float32).astype(BF)
    u = d["u"].reshape(N, 128, 128, 4)
    u[:, :, ::16] = 0
    for r in range(N):
        for h in range(0, 128, 16): u[r, h, h, 0] = 0.0 if r == o[0] else -1.0 if r == o[1] else 1.0
    return {"x": x.reshape(N, 128, 4 * C), "u": u.reshape(N, 128, 512), "v": d["v"], **stored(a, m), **weights(rng, layers(rng, [0]))}
def setup_inputs_near(rng):
    d = numbers_of(rng)
    x = d["x"].astype(np.float32).reshape(N, 8, 16, C, 4)
    x[:, :, 0] = 0
    x[:, :, 8:] = 0
    x[:, :, 15, :, 0] = 2.0 ** -26
    u = d["u"].reshape(N, 128, 128, 4)
    u[:, :, ::16] = 0
    o = rng.permutation(N) % 4
    for r in range(N):
        c = rng.choice([-1.0, 1.0], (8, 1))
        s = rng.integers(0, 16, (8, C))
        digits = ((s[:, :, None] >> np.arange(4)) & 1) * np.exp2(np.arange(4) - 23.0)
        if o[r] < 2:
            x[r, :, 0, :, 0] = c
            x[r, :, 8] = digits
            x[r, :, 11, :, 0] = 2.0 ** -10
        elif o[r] == 2: x[r, :, 8] = digits * rng.choice([-1.0, 1.0], (8, C, 1))
        else:
            x[r, :, 8, :, 0] = np.where(s < 8, 1.25, 0.0) * 2.0 ** -30 * c
            x[r, :, 9, :, 0] = np.where(s < 8, 0.0, 1.125) * 2.0 ** -30 * c
            for g in rng.permutation(8)[:4]:
                e = rng.choice([-1.0, 1.0], C) * 2.0 ** -30
                x[r, g, 8, :, 0] = 1.25 * e
                x[r, g, 9, :, 0] = -1.125 * e
            x[r, :, 13, :, 0] = rng.choice([-1.0, 1.0], (8, C)) * 2.0 ** -30
        at = [0, C - 1, int(rng.integers(C)), int(rng.integers(C))]
        for g, j in zip(rng.permutation(8)[:4], at): x[r, g, 0, j, 0] = 2.0 ** 29 * rng.choice([-1.0, 1.0])
        k = 1.0 if o[r] == 0 else 2.0 ** -30
        for h in range(0, 128, 16):
            u[r, h, h, 0] = k if o[r] < 2 else 1.0
            if o[r] < 2: u[r, h + 11, h, 0] = k
            if o[r] < 3: u[r, h + 8, h] = k
            else:
                u[r, h + 8, h, 0] = k
                u[r, h + 9, h, 0] = 1.125 * k
                u[r, h + 14, h, 0] = k
    w = layers(rng, [0, 8, 9, 10, 11, 12, 13, 14, 15])
    for g in range(8): w[:, g, 13, 0, g, 14, 0] = 2.0 ** -5
    return {"x": x.reshape(N, 128, 4 * C).astype(BF), "u": u.reshape(N, 128, 512), "v": d["v"], **stored(*lists(rng)), **weights(rng, w)}
def setup_inputs_odd(rng):
    d = numbers_of(rng)
    x = (1.0 + (2 * rng.integers(0, 64, (N, 16, 8, C, 4)) + 1) * 2.0 ** -7) * np.exp2(-rng.integers(0, 7, (N, 16, 8, C, 4)).astype(np.float64)) * rng.choice([-1.0, 1.0], (N, 16, 8, C, 4))
    x[:, :, 0, :, 0] = (np.where((parity()[:, None] + np.arange(16)) % 2 == 0, 1.96875, 1.875) * 2.0 ** 8)[:, :, None]
    x[:, :, 1, :, 0] = rng.integers(8, 16, (N, 16, C)) * 2.0 ** -8
    u = d["u"].reshape(N, 16, 8, 128, 4)
    u[:, :, 0, ::16] = 0
    for r in range(N):
        for g in rng.permutation(8)[:2]:
            u[r, :, :, 16 * g] = 0
            u[r, 2 * g + parity()[r], 1, 16 * g, 0] = 1.0
    w = layers(rng, [0, 1, 8, 9])
    for g in range(8):
        for i in (0, 8): w[:, g, i, 0, g, i, 0] = -0.5
    return {"x": x.astype(np.float32).reshape(N, 128, 4 * C).astype(BF), "u": u.reshape(N, 128, 512), "v": d["v"], **stored(*lists(rng)), **weights(rng, w)}
def setup_inputs_ends(rng):
    d = numbers_of(rng)
    r0 = int(rng.integers(N))
    a = rng.permutation(np.array([r0, r0 ^ STEP[0], r0 ^ STEP[1], r0 ^ STEP[0] ^ STEP[1]]))
    z = rng.permutation(np.setdiff1d(np.arange(N), a))
    x = np.where(rng.random((N, 128, C, 4)) < 0.5, -1.0, -0.9375) * 2.0 ** 30
    x[:, 5] *= 2.0 ** -10
    c = rng.choice([-1.0, 1.0], (128, 1, 4))
    for r in z[:2]: x[r] = c * (1.0 + 0.125 * rng.integers(0, 8, (128, C, 4))) * 2.0 ** -30
    for r in z[2:]: x[r] = x[r] * rng.choice([-1.0, 1.0], (1, C, 1))
    size = np.full(N, 2.0 ** 30)
    size[a[2:]] = 2.0 ** -30
    size[z[1::2]] = 2.0 ** -30
    u = d["u"].astype(np.float32).reshape(N, 128, 128, 4)
    w = np.zeros((N, 128, 4, 128, 4), np.float32)
    i = np.arange(128)
    for b in range(4): w[:, i, b, i, b] = 32.0
    w[a[2], 5, 0, 5, 0] = 2.0 ** 8
    w[a[2], 6, 0, 6, 0] = 2.0 ** -8
    k = np.array([[0, 0, 2, 2, 1, 1, 3, 3], [2, 1, 0, 3, 0, 3, 2, 1]])[parity()][:, rng.permutation(8)]
    e, m = lists(rng)
    j = np.arange(C)
    for r in range(N):
        h = rng.permutation(8)
        u[r, :, ::16] = (np.where(h < 2, 0.0, h % 2 * 2.0 - 1.0) * size[r])[None, :, None]
        for g in range(8):
            t = int(rng.integers(4))
            if t: m[r, g] = [C - 1 - j, j ^ 1, (j + H) % C][t - 1]
            e[r, g] = [ring(rng.permutation(C)), j, ring(j), m[r, g]][k[r, g]]
    u[:, 5, ::16] = 0
    v = rng.choice([-1.0, 1.0], (N, 128, 512)) * size[:, None, None]
    return {"x": x.astype(np.float32).reshape(N, 128, 4 * C).astype(BF), "u": u.reshape(N, 128, 512).astype(BF), "v": v.astype(np.float32).astype(BF), **stored(e, m), **weights(rng, w.astype(BF))}
def setup_inputs_spread(rng):
    d = setup_inputs(rng)
    d["x"] = wide(rng, N, 128, 4 * C, cols=6)
    return d
def check_inputs(d):
    b = []
    for k in ("x", "u", "v"):
        a = np.abs(d[k].astype(np.float32))
        if not (np.isfinite(a).all() and ((a == 0) | (a >= 2.0 ** -30) & (a <= 2.0 ** 30)).all()): b.append("a value of " + k)
    none, least, most = [emit(mx_ref.quantize(np.full((128, 16), k, np.float32).astype(BF)))[1][0, 0] for k in (0.0, 2.0 ** -8, 2.0 ** 8)]
    for r in range(N):
        if (np.sort(gentries(d["fl"][r]), axis=1) != OWN).any(): b.append("fl: a group that doesn't name every column once")
        m = gentries(d["ml"][r])
        if ((m < 0) | (m >= C)).any() or (m == OWN).any() or (m[G, m] != OWN).any(): b.append("ml: columns that aren't each other's mates")
        if ((d["wc"][r] == 0x7F) | (d["wc"][r] == 0xFF)).any(): b.append("wc: a code that is no number")
        s = mx_ref.live(d["ws"][r])
        if ((s != none) & ((s < least) | (s > most))).any(): b.append("ws: a scale out of range")
    return b
def leaders(a, s):
    best, w = OWN, a
    for _ in range(C - 1):
        p, o = s[G, w], s[G, best]
        best = np.where((p > o) | (p == o) & (w < best), w, best)
        w = a[G, w]
    return best
def hops(a, best):
    n, w = np.zeros((8, C), np.int64), best
    for _ in range(C - 1):
        go = w != OWN
        n, w = n + go, np.where(go, a[G, w], w)
    return n
def walk(a, at, n):
    for i in range(C - 1): at = np.where(i < n, a[G, at], at)
    return at
def reference(x, u, v, fl, ml, wc, ws):
    qu = [mx_ref.quantize(u[r]) for r in range(N)]
    lay = [pk(wc[r], ws[r]) for r in range(N)]
    cyc, mate = [gentries(fl[r]) for r in range(N)], [gentries(ml[r]) for r in range(N)]
    now = [x[r] for r in range(N)]
    for step in STEP:
        q = [mx_ref.quantize(now[r]) for r in range(N)]
        t = [decode(q[r]).astype(BF) for r in range(N)]
        made, after = [], []
        for r in range(N):
            p = r ^ step
            s = mx_ref.matmul(qu[r], q[r])[::16] + np.float32(0.0)
            lead = leaders(cyc[r], s)
            far = walk(cyc[p], lead, hops(cyc[r], lead))
            mine = s[G, far]
            other = mine[G, mate[r]]
            swap = np.where(OWN < mate[r], mine < other, other < mine)
            new = cyc[r][G, np.where(swap, mate[r], OWN)]
            back = np.argsort(new, axis=1)
            z = mx_ref.quantize(((gcols(t[r], new).astype(np.float32) + gcols(t[p], far).astype(np.float32)) * np.float32(0.5)).astype(BF))
            res = [mx_ref.matmul(pick(lay[r], np.arange(128 * b, 128 * b + 128)), z) * np.float32(0.03125) for b in range(4)]
            made.append(tile([(t[r][:, b::4].astype(np.float32) + gpick(res[b], back)) * np.float32(0.5) for b in range(4)]))
            after.append(new)
        now, cyc = made, after
    y, nl = np.zeros((N, 128, C), np.float32), np.zeros((N, 8, C), np.float32)
    oc, osc = np.zeros((N, 128, 4 * C), np.uint8), np.zeros((N, 16, C), np.uint8)
    for r in range(N):
        q = mx_ref.quantize(now[r])
        y[r] = mx_ref.matmul(mx_ref.quantize(v[r]), q)
        nl[r] = cyc[r]
        oc[r], osc[r] = emit(q)
    return {"y": y, "nl": nl, "oc": oc, "osc": osc}

@@ -1,0 +1,541 @@
+from concourse.mybir import dt, AluOpType, ActivationFunctionType
+
+A = AluOpType
+COPY = ActivationFunctionType.Copy
+IDENT = ActivationFunctionType.Identity
+C = 288
+TC = C // 16
+MASKS = [4, 1, 2]
+LEVELS = [(3, 1), (3, 3), (2, 9), (2, 18), (2, 36), (2, 72), (2, 144)]
+PARTS = {"a": (0, 160), "b": (160, C)}
+Z_HOME = ()
+TWIN_HOME = ()
+R_HOME = (0, 1)
+WAKE, GATHER, EL = 0.06, 1.5e-3, 1.04e-3
+LOOK, EDGE = 0.5, 0.3
+NE, NL = 8, 2
+NMK = 6
+
+SCRATCH = {}
+
+
+def _b(names, n, dtype, where="sbuf"):
+    for name in names.split():
+        SCRATCH[name] = (where, [128, n], dtype)
+
+
+CODE = "float8_e4m3fn_x4"
+_b("x0 xt z fh fs gt", 4 * C, "bfloat16")
+_b("rb gp", 4 * C, "float32")
+_b("xq0 xq1 xq2 xq3 lc0 lc1 lc2 zq", C, CODE)
+_b("xs0 xs1 xs2 xs3 ls0 ls1 ls2 zs", C, "uint8")
+_b("fo0 fo1 fo2 fo3 lo0 lo1 lo2 w1 w2 w3 to mo loo hio eo8 eo64 so", TC, "uint16")
+_b("wq eq", 512, CODE)
+_b("wsp eqs", 512, "uint8")
+_b("uq uk vq", 128, CODE)
+_b("uqs uks vqs", 128, "uint8")
+_b("et", 2048, "bfloat16")
+_b("ub vb", 512, "bfloat16")
+_b("fli mli ki ka k0 k1 k2 x1 o1", TC, "int32")
+_b("jf j16 key s s2 mc0 mc1 m0 m1 m2 y0 y1 y2 y3 za0 za1 zb0 zb1 mine mhi km ks yb nlr mbig", C, "float32")
+_b("jc mask keep frow srow cand", C, "bfloat16")
+_b("mk sc", NMK * C, "bfloat16")
+_b("hr", 8 * C, "bfloat16")
+_b("er", 21 * C, "bfloat16")
+_b("ho", 7 * TC, "uint16")
+_b("uo", 8, "uint16")
+_b("c16 jt mtf lof hif ffc dfm dmt ta tb tb2 tc x2 x3 o2 o3", TC, "float32")
+_b("pi p16i", 2, "int32")
+_b("pf p16", 2, "float32")
+_b("p0 p1 p2 p3 p4 p5 p6 p7", 512, "float32", "psum")
+
+SEMAPHORES = ["cv", "cs", "ct", "cp", "lx", "lu", "lv", "lf", "lm", "lw", "lq", "lout", "sent"]
+SEMAPHORES += ["ac%d" % r for r in range(3)] + ["al%d" % r for r in range(3)]
+
+
+def relay_of(src, dst, topo):
+    if topo.may_write(src, dst):
+        return None
+    cs = [c for c in topo.cores_of(src) if topo.may_write(c, dst)]
+    near = [c for c in cs if topo.die(c) == topo.die(src)]
+    return (near or cs)[0]
+
+
+def send(g, T, topo, src, dst, out_ap, in_ap, sem, count):
+    rid, pid = topo.addr(dst, src)
+    e = topo.engines(src, dst)[:count]
+    m = 0
+    for k in e:
+        m |= 1 << k
+    g.remote_dma(out_ap=out_ap, in_ap=in_ap, remote_sem=T.sem[sem], local_sem=T.sem.sent, pid=pid, routing_id=rid,
+                 dma_engine_mask=m)
+    return len(e)
+
+
+def order(ops):
+    n = len(ops)
+    users = [[] for _ in range(n)]
+    for i, o in enumerate(ops):
+        for d in o["deps"]:
+            users[d].append(i)
+    far = [0.0] * n
+    for i in range(n - 1, -1, -1):
+        o = ops[i]
+        far[i] = o["c"] + o["tail"] + max([far[u] + WAKE for u in users[i]] or [0.0])
+    left = [len(o["deps"]) for o in ops]
+    ready = [0.0] * n
+    end = [0.0] * n
+    open_ = {}
+    free = {}
+    out = []
+
+    def finish(i, t):
+        end[i] = t
+        for u in users[i]:
+            left[u] -= 1
+            ready[u] = max(ready[u], t if ops[i]["q"] == ops[u]["q"] and not ops[i]["tail"] and ops[i]["free"] else t + WAKE)
+            if left[u] == 0:
+                release(u)
+
+    def release(u):
+        if ops[u]["q"] is None:
+            out.append(u)
+            finish(u, ready[u] + ops[u]["tail"])
+        else:
+            open_.setdefault(ops[u]["q"], []).append(u)
+
+    for i in range(n):
+        if not ops[i]["deps"]:
+            release(i)
+    while any(open_.values()):
+        pick = None
+        for q, cand in open_.items():
+            if not cand:
+                continue
+            t = max(free.get(q, 0.0), min(ready[i] for i in cand))
+            now = [i for i in cand if ready[i] <= t + 1e-9]
+            b = max(now, key=lambda i: (far[i], -i))
+            stop = t + ops[b]["c"]
+            for i in cand:
+                if far[i] > far[b] + EDGE and ready[i] < stop and ready[i] - t < LOOK * (stop - ready[i]):
+                    b = i
+            s = max(t, ready[b])
+            if pick is None or s < pick[0]:
+                pick = (s, q, b)
+        s, q, b = pick
+        open_[q].remove(b)
+        free[q] = s + ops[b]["c"]
+        out.append(b)
+        finish(b, free[q] + ops[b]["tail"])
+    return out
+
+
+def rank_program(g, core, T, topo):
+    rank = T.rank_of(core)
+    if rank is None:
+        relay_program(g, core, T, topo)
+        return
+    queues = {"v": g.vector, "s": g.scalar, "t": g.tensor, "p": g, "y": g.sync}
+    own = {"v": "cv", "s": "cs", "t": "ct", "p": "cp"}
+    V, S, P = g.vector, g.scalar, g.tensor
+    ops = []
+    acc = {}
+
+    def op(qn, rd, wr, fn, cost, sem=None, inc=1, tail=0.0, ev=None):
+        deps = set()
+        me = len(ops)
+        for r in rd:
+            a = acc.setdefault(r, [None, []])
+            if a[0] is not None:
+                deps.add(a[0])
+        for r in wr:
+            a = acc.setdefault(r, [None, []])
+            deps.update(a[1])
+            if a[0] is not None:
+                deps.add(a[0])
+        for r in rd:
+            acc[r][1].append(me)
+        for r in wr:
+            acc[r] = [me, []]
+        deps.discard(me)
+        ops.append(dict(q=qn, c=cost, tail=tail, deps=deps, fn=fn, sem=sem or own.get(qn), inc=inc, ev=ev, free=False))
+        return me
+
+    def emit():
+        total, know = {}, {k: {} for k in queues}
+        for i in order(ops):
+            o = ops[i]
+            if o["q"] is None:
+                o["knows"] = {}
+                continue
+            k = know[o["q"]]
+            waits = sorted((ops[d]["ev"] + (d,) for d in o["deps"] if ops[d]["ev"]), key=lambda e: -len(ops[e[2]]["knows"]))
+            top = {}
+            for s, n, d in waits:
+                if n > top.get(s, (0,))[0]:
+                    top[s] = (n, d)
+            for s, n, d in waits:
+                if top[s] != (n, d) or k.get(s, 0) >= n:
+                    continue
+                queues[o["q"]].wait_ge(T.sem[s], n)
+                for a, b in ops[d]["knows"].items():
+                    if k.get(a, 0) < b:
+                        k[a] = b
+                k[s] = n
+            if o["sem"] is None:
+                o["fn"]()
+                o["knows"] = {}
+                continue
+            total[o["sem"]] = total.get(o["sem"], 0) + o["inc"]
+            o["fn"]().then_inc(T.sem[o["sem"]], o["inc"])
+            o["ev"] = (o["sem"], total[o["sem"]])
+            o["knows"] = dict(k)
+            o["knows"][o["sem"]] = total[o["sem"]]
+        for s in sorted(total):
+            if know["p"].get(s, 0) < total[s]:
+                g.wait_ge(T.sem[s], total[s])
+        g.wait_ge(T.sem.sent, sends[0])
+
+    def el(n, k=1.0):
+        return max(n * k, 64) * EL
+
+    def ga(n):
+        return 0.055 + n * GATHER
+
+    def ts(out, ow, in0, ir, s1, o1, s2=None, o2=None, n=TC):
+        if o2 is None:
+            op("v", ir, ow, lambda: V.tensor_scalar(out, in0, s1, None, o1), el(n))
+        else:
+            op("v", ir, ow, lambda: V.tensor_scalar(out, in0, s1, s2, o1, o2), el(n))
+
+    def tt(out, ow, a, b, ir, o, c=None):
+        op("v", ir, ow, lambda: V.tensor_tensor(out, a, b, o), el(TC) if c is None else c)
+
+    def cp(out, ow, a, ir, c=None):
+        op("v", ir, ow, lambda: V.tensor_copy(out, a), el(TC) if c is None else c)
+
+    def sg(out, ow, a, ir, c=None, scale=None):
+        c = ga(C) if c is None else c
+        if scale is None:
+            op("s", ir, ow, lambda: S.activation(out, a, COPY), c)
+        else:
+            op("s", ir, ow, lambda: S.activation(out, a, COPY, scale=scale), c)
+
+    def lin(out, ow, a, ir, scale, bias, n=C):
+        op("s", ir, ow, lambda: S.activation(out, a, IDENT, bias=float(bias), scale=float(scale)), el(n))
+
+    def hslot(k):
+        return T.hr[:, k * C:(k + 1) * C], "hr%d" % k
+
+    def eslot(k):
+        return T.er[:, k * C:(k + 1) * C], "er%d" % k
+
+    def htab(k):
+        return T.ho[:, k * TC:(k + 1) * TC], "ho%d" % k
+
+    rot = [0]
+
+    def turn_mk():
+        k = rot[0] % NMK
+        rot[0] += 1
+        return T.mk[:, k * C:(k + 1) * C], "mk%d" % k, k, "sc%d" % k
+
+    def scan(mk, mr, k, sr):
+        op("v", [mr, "keep"], [sr],
+           lambda: V.tensor_tensor_scan(T.sc[:, k * C:(k + 1) * C], T.keep[:, :], mk, 0.0, A.mult, A.add), el(C, 0.5))
+        return T.sc[:, k * C + 15:(k + 1) * C:16], sr
+
+    def conv(win, wr, off, orr):
+        mk, mr, sc, sr = turn_mk()
+        tt(mk, [mr], win.indirect(off), T.mask[:, :], wr + [orr, "mask"], A.mult, ga(C))
+        return scan(mk, mr, sc, sr)
+
+    def to_off(out, ow, view, vr):
+        ts(out, [ow], view, [vr], float(C // 2), A.add)
+
+    def mm(bank, st, sts, sr, mv, mvs, mr):
+        op("t", sr + mr, [bank], lambda: P.matmul_mx(T[bank][:, 0:C], st, sts, mv, mvs, True, True), 0.3)
+
+    def quant(q, s, rd, wr, src, n):
+        op("v", rd, wr, lambda: V.quantize_mx(q, s, src), 0.012 + 0.28e-3 * n)
+
+    def load(qn, out, in_, res, sem, tail=2.0):
+        op(qn, [], [res], lambda: queues[qn].dma_start(out=out, in_=in_), 0.1, sem, 16, tail)
+
+    sends = [0]
+
+    def to_partner(r, bufs, sem, count, n, land, tail):
+        dst = T.cores[rank ^ MASKS[r]]
+        via = relay_of(core, dst, topo)
+        hop = dst if via is None else via
+        ids = []
+
+        def go(o, i):
+            sends[0] += send(g, T, topo, core, hop, o, i, sem, count)
+
+        for o, i, res in bufs:
+            op("p", [res], ["out" + sem], lambda o=o, i=i: go(o, i), 0.5)
+            ops[-1]["sem"] = None
+        op(None, ["out" + sem], [land], None, 0.0, None, 0, tail if via is None else 2 * tail, (sem, n))
+
+    def send_list(r):
+        to_partner(r, [(T["lo%d" % r][:, :], T["fo%d" % r][:, :], "fo%d" % r)], "al%d" % r, NL, NL, "lo%d" % r, 4.0)
+
+    def send_codes(r):
+        to_partner(r, [(T["lc%d" % r][:, :].bitcast(dt.uint8), T["xq%d" % r][:, :].bitcast(dt.uint8), "xq%d" % r),
+                       (T["ls%d" % r][:, :], T["xs%d" % r][:, :], "xq%d" % r)], "ac%d" % r, NE, 2 * NE, "lc%d" % r, 7.0)
+
+    load("y", T.fli[:, :], T.fl[:, :], "fli", "lf")
+    load("s", T.x0[:, :], T.x[:, :], "x0", "lx", 3.0)
+    load("y", T.ub[:, :], T.u[:, :], "ub", "lu")
+    load("y", T.mli[:, :], T.ml[:, :], "mli", "lm")
+    load("y", T.wq[:, :].bitcast(dt.uint8), T.wc[:, :], "wq", "lw")
+    load("y", T.wsp[:, :], T.ws[:, :], "wsp", "lq")
+    load("y", T.vb[:, :], T.v[:, :], "vb", "lv")
+
+    def iota(name, pattern, mult, n, flag=True):
+        if flag:
+            op("p", [], [name], lambda: g.iota(T[name][:, :], pattern, 0, mult, allow_small_or_imprecise_dtypes=True),
+               0.13 + 2 * n * EL)
+        else:
+            op("p", [], [name], lambda: g.iota(T[name][:, :], pattern, 0, mult), 0.13 + 2 * n * EL)
+
+    iota("pi", [[0, 2]], 1, 2, False)
+    iota("j16", [[0, TC], [1, 16]], 0, C)
+    iota("jf", [[1, C]], 0, C)
+    iota("c16", [[16, TC]], 0, TC)
+    op("v", [], ["et"], lambda: V.memset(T.et[:, :], 0.0), 0.9)
+    ts(T.p16i[:, :], ["p16i"], T.pi[:, :], ["pi"], 15, A.bitwise_and)
+    cp(T.pf[:, :], ["pf"], T.pi[:, :], ["pi"])
+    cp(T.p16[:, :], ["p16"], T.p16i[:, :], ["p16i"])
+    ts(T.keep[:, :], ["keep"], T.j16[:, :], ["j16"], 1.0, A.min, n=C)
+    ts(T.mask[:, :], ["mask"], T.j16[:, :], ["j16", "p16"], T.p16[:, 0:1], A.is_equal, n=C)
+    ts(T.jc[:, :], ["jc"], T.jf[:, :], ["jf"], float(-(C // 2)), A.add, n=C)
+    for k in (7, 15, 20):
+        sg(eslot(k)[0], [eslot(k)[1]], T.jc[:, :], ["jc"], el(C))
+    lin(T.mbig[:, :], ["mbig"], T.mask[:, :], ["mask"], 2e29, -1e29)
+    lin(T.key[:, :], ["key"], T.jf[:, :], ["jf"], -512.0, 512 * C + 224)
+
+    cp(T.fo0[:, :], ["fo0"], T.fli[:, :], ["fli"])
+    send_list(0)
+    op("v", ["jc", "fo0"], ["hr0"], lambda: V.tensor_copy(T.hr[:, 0:C].indirect(T.fo0[:, :]), T.jc[:, :]), 1.0)
+    mk, mr, sc, sr = turn_mk()
+    tt(mk, [mr], T.hr[:, 0:C], T.mask[:, :], ["hr0", "mask"], A.mult, el(C, 2))
+    to_off(htab(0)[0], "ho0", *scan(mk, mr, sc, sr))
+    ts(T.ffc[:, :], ["ffc"], T.fli[:, :], ["fli"], float(-(C // 2)), A.add)
+
+    quant(T.xq0[:, :], T.xs0[:, :], ["x0"], ["xq0"], T.x0[:, :], 4 * C)
+    send_codes(0)
+    quant(T.uq[:, :], T.uqs[:, :], ["ub"], ["uq"], T.ub[:, :], 512)
+    cp(T.uo[:, :], ["uo"], T.c16[:, 0:8], ["c16"])
+    cp(T.uk[:, :].bitcast(dt.uint32), ["uk"], T.uq[:, :].bitcast(dt.uint32).indirect(T.uo[:, :]), ["uq", "uo"], ga(128))
+    cp(T.uks[:, :], ["uks"], T.uqs[:, :].indirect(T.uo[:, :]), ["uq", "uo"], ga(128))
+    for b in range(4):
+        lo = 512 * b
+        ts(T.et[:, lo + b:lo + 512:4], ["et%d" % b], T.jf[:, 0:128], ["jf", "pf", "et"], T.pf[:, 0:1], A.is_equal,
+           0.5, A.mult, n=128)
+    quant(T.eq[:, :], T.eqs[:, :], ["et", "et0", "et1", "et2", "et3"], ["eq"], T.et[:, :], 2048)
+    cp(T.mo[:, :], ["mo"], T.mli[:, :], ["mli"])
+    cp(T.mtf[:, :], ["mtf"], T.mli[:, :], ["mli"])
+    ts(T.jt[:, :], ["jt"], T.c16[:, :], ["c16", "p16"], T.p16[:, 0:1], A.add)
+    tt(T.lof[:, :], ["lof"], T.mtf[:, :], T.jt[:, :], ["mtf", "jt"], A.min)
+    tt(T.hif[:, :], ["hif"], T.mtf[:, :], T.jt[:, :], ["mtf", "jt"], A.max)
+    tt(T.dmt[:, :], ["dmt"], T.mtf[:, :], T.jt[:, :], ["mtf", "jt"], A.subtract)
+    cp(T.loo[:, :], ["loo"], T.lof[:, :], ["lof"])
+    cp(T.hio[:, :], ["hio"], T.hif[:, :], ["hif"])
+
+    def hrow(k, frm, tab):
+        w, wr = (T.jc[:, :], "jc") if frm is None else hslot(frm)
+        o, orr = htab(tab)
+        sg(hslot(k)[0], [hslot(k)[1]], w.indirect(o), [wr, orr])
+
+    def hconv(frm, tab, new):
+        w, wr = hslot(frm)
+        o, orr = htab(tab)
+        to_off(*htab(new), *conv(w, [wr], o, orr))
+
+    def erow(k, off, orr):
+        w, wr = eslot(k + 1)
+        sg(eslot(k)[0], [eslot(k)[1]], w.indirect(off), [wr, orr])
+
+    for r in range(3):
+        last = r == 2
+        xq, xs, xr = T["xq%d" % r], T["xs%d" % r], ["xq%d" % r]
+        eo, eor = T["lo%d" % r][:, :], "lo%d" % r
+        mm("p4", T.uk[:, :], T.uks[:, :], ["uk", "uks"], xq[:, :], xs[:, :], xr)
+        mm("p5", T.uk[:, :], T.uks[:, :], ["uk", "uks"], xq[:, :], xs[:, :], xr)
+        sg(T.s[:, :], ["s", "p4"], T.p4[:, 0:C], [], el(C))
+        cp(T.s2[:, :], ["s2", "p5"], T.p5[:, 0:C], [], el(C))
+        for b in range(4):
+            mm("p%d" % b, T.eq[:, 128 * b:128 * b + 128], T.eqs[:, 128 * b:128 * b + 128], ["eq"], xq[:, :], xs[:, :], xr)
+        if r:
+            hrow(0, None, 0)
+        hrow(1, 0, 0)
+        hrow(2, 1, 0)
+        hconv(1, 0, 1)
+        hrow(3, 2, 1)
+        for k in range(5):
+            hconv(3 + k, 1 + k, 2 + k)
+            if k < 4:
+                hrow(4 + k, 3 + k, 1 + k)
+        if r == 0:
+            sg(T.frow[:, :], ["frow"], T.jc[:, :].indirect(T.fo0[:, :]), ["jc", "fo0"])
+            v, vr = conv(T.frow[:, :], ["frow"], T.mo[:, :], "mo")
+            tt(T.dfm[:, :], ["dfm"], v, T.ffc[:, :], [vr, "ffc"], A.subtract)
+        for k in range(6, -1, -1):
+            erow(k, eo, eor)
+        to_off(T.eo8[:, :], "eo8", *conv(eslot(0)[0], [eslot(0)[1]], eo, eor))
+        for k in range(14, 7, -1):
+            erow(k, T.eo8[:, :], "eo8")
+        to_off(T.eo64[:, :], "eo64", *conv(eslot(8)[0], [eslot(8)[1]], T.eo8[:, :], "eo8"))
+        for k in range(19, 15, -1):
+            erow(k, T.eo64[:, :], "eo64")
+
+        cur = "s"
+        turn = 0
+        for level, (rad, n) in enumerate(LEVELS):
+            o, orr = htab(level)
+            base, side = cur, "s2"
+            if level:
+                side = "mc%d" % (level % 2)
+                if level in TWIN_HOME:
+                    cp(T[side][:, :], [side], T[cur][:, :], [cur], el(C))
+                else:
+                    sg(T[side][:, :], [side], T[cur][:, :], [cur], el(C))
+            for i in range(rad - 1):
+                d = "m%d" % (turn % 3)
+                turn += 1
+                z = base if i else side
+                tt(T[d][:, :], [d], T[cur][:, :].indirect(o), T[z][:, :], [cur, z, orr], A.max, ga(C))
+                cur = d
+        tt(T.cand[:, :], ["cand", "p5"], T[cur][:, :], T.p5[:, 0:C], [cur], A.is_equal, el(C))
+        for p, (lo, hi) in PARTS.items():
+            tt(T.y0[:, lo:hi], ["y0" + p], T.cand[:, lo:hi], T.key[:, lo:hi], ["cand", "key"], A.mult, el(hi - lo, 2))
+        cur = "y0"
+        turn = 1
+        for level, (rad, n) in enumerate(LEVELS):
+            orr = htab(level)[1]
+            base = cur
+            for i in range(rad - 1):
+                zz = "z%s%d" % ("ab"[i], level % 2)
+                for p, (lo, hi) in PARTS.items():
+                    if level in Z_HOME:
+                        ts(T[zz][:, lo:hi], [zz + p], T[base][:, lo:hi], [base + p], float(n * (i + 1)), A.add, n=hi - lo)
+                    else:
+                        lin(T[zz][:, lo:hi], [zz + p], T[base][:, lo:hi], [base + p], 1.0, n * (i + 1), hi - lo)
+            for i in range(rad - 1):
+                zz = "z%s%d" % ("ab"[i], level % 2)
+                d = "y%d" % (turn % 4)
+                turn += 1
+                for p, (lo, hi) in PARTS.items():
+                    off = T.ho[:, level * TC + lo // 16:level * TC + hi // 16]
+                    tt(T[d][:, lo:hi], [d + p], T[cur][:, :].indirect(off), T[zz][:, lo:hi],
+                       [cur + q for q in PARTS] + [zz + p, orr], A.max, ga(hi - lo))
+                cur = d
+        for b in range(4):
+            sg(T.fh[:, b * C:(b + 1) * C], ["fh%d" % b, "p%d" % b], T["p%d" % b][:, 0:C], [], el(C))
+        for b in range(4):
+            mm("p%d" % (4 + b), T.eq[:, 128 * b:128 * b + 128], T.eqs[:, 128 * b:128 * b + 128], ["eq"],
+               T["lc%d" % r][:, :], T["ls%d" % r][:, :], ["lc%d" % r])
+            sg(T.fs[:, b * C:(b + 1) * C], ["fs%d" % b, "p%d" % (4 + b)], T["p%d" % (4 + b)][:, 0:C], [], el(C))
+
+        tt(T.km[:, :], ["km"], T[cur][:, :], T.mask[:, :], [cur + p for p in PARTS] + ["mask"], A.mult, el(C, 2))
+        op("v", ["km", "keep"], ["ks"],
+           lambda: V.tensor_tensor_scan(T.ks[:, :], T.keep[:, :], T.km[:, :], 0.0, A.mult, A.add), el(C))
+        cp(T.ki[:, :], ["ki"], T.ks[:, 15:C:16], ["ks"])
+        ts(T.k0[:, :], ["k0"], T.ki[:, :], ["ki"], 7, A.bitwise_and)
+        ts(T.ka[:, :], ["ka"], T.ki[:, :], ["ki"], 9, A.logical_shift_right)
+        ts(T.k1[:, :], ["k1"], T.ki[:, :], ["ki"], 3, A.logical_shift_right, 7, A.bitwise_and)
+        ts(T.x1[:, :], ["x1"], T.k0[:, :], ["k0"], float(C), A.mult, float(C), A.add)
+        ts(T.k2[:, :], ["k2"], T.ki[:, :], ["ki"], 6, A.logical_shift_right, 7, A.bitwise_and)
+        tt(T.o1[:, :], ["o1"], T.x1[:, :], T.ka[:, :], ["x1", "ka"], A.subtract)
+        ts(T.x2[:, :], ["x2"], T.k1[:, :], ["k1"], float(C), A.mult, float(C // 2), A.add)
+        ts(T.x3[:, :], ["x3"], T.k2[:, :], ["k2"], float(C), A.mult, float(C // 2 - 3 * C), A.add)
+        cp(T.w1[:, :], ["w1"], T.o1[:, :], ["o1"])
+        v, vr = conv(T.er[:, 0:8 * C], ["er%d" % k for k in range(8)], T.w1[:, :], "w1")
+        tt(T.o2[:, :], ["o2"], T.x2[:, :], v, ["x2", vr], A.add)
+        cp(T.w2[:, :], ["w2"], T.o2[:, :], ["o2"])
+        v, vr = conv(T.er[:, 8 * C:16 * C], ["er%d" % k for k in range(8, 16)], T.w2[:, :], "w2")
+        tt(T.o3[:, :], ["o3"], T.x3[:, :], v, ["x3", vr], A.add)
+        cp(T.w3[:, :], ["w3"], T.o3[:, :], ["o3"])
+        to_off(T.to[:, :], "to", *conv(T.er[:, 16 * C:21 * C], ["er%d" % k for k in range(16, 21)], T.w3[:, :], "w3"))
+
+        for b in range(4):
+            sg(T.gt[:, b * C:(b + 1) * C], ["gt%d" % b], T.fs[:, b * C:(b + 1) * C].indirect(T.to[:, :]),
+               ["fs%d" % b, "to"])
+        nfo, nfr = T["fo%d" % (r + 1)], "fo%d" % (r + 1)
+        cp(T.mine[:, :], ["mine"], T.s[:, :].indirect(T.to[:, :]), ["s", "to"], ga(C))
+        tt(T.mhi[:, :], ["mhi"], T.mine[:, :].indirect(T.hio[:, :]), T.mbig[:, :], ["mine", "hio", "mbig"], A.min, ga(C))
+        mk, mr, sc, sr = turn_mk()
+        tt(mk, [mr], T.mine[:, :].indirect(T.loo[:, :]), T.mhi[:, :], ["mine", "mhi", "loo"], A.is_lt, ga(C))
+        v, vr = scan(mk, mr, sc, sr)
+        tt(T.ta[:, :], ["ta"], v, T.dfm[:, :], [vr, "dfm"], A.mult)
+        tt(T.tb[:, :], ["tb"], v, T.dmt[:, :], [vr, "dmt"], A.mult)
+        tt(T.ffc[:, :], ["ffc"], T.ta[:, :], T.ffc[:, :], ["ta"], A.add)
+        to_off(nfo[:, :], nfr, T.ffc[:, :], "ffc")
+        if not last:
+            send_list(r + 1)
+            ts(T.tc[:, :], ["tc"], T.ta[:, :], ["ta"], -2.0, A.mult)
+            tt(T.dfm[:, :], ["dfm"], T.tc[:, :], T.dfm[:, :], ["tc"], A.add)
+        tt(T.tb2[:, :], ["tb2"], T.tb[:, :], T.jt[:, :], ["tb", "jt"], A.add)
+        cp(T.so[:, :], ["so"], T.tb2[:, :], ["tb2"])
+        sg(T.srow[:, :], ["srow"], T.jc[:, :].indirect(T.so[:, :]), ["jc", "so"])
+        o, orr = htab(0)
+        to_off(o, orr, *conv(T.srow[:, :], ["srow"], o, orr))
+        for b in range(4):
+            tt(T.z[:, b:4 * C:4], ["z%d" % b], T.fh[:, b * C:(b + 1) * C].indirect(nfo[:, :]),
+               T.gt[:, b * C:(b + 1) * C], ["fh%d" % b, "gt%d" % b, nfr], A.add, ga(C))
+        quant(T.zq[:, :], T.zs[:, :], ["z0", "z1", "z2", "z3"], ["zq"], T.z[:, :], 4 * C)
+        for b in (2, 3, 0, 1):
+            bank = "p%d" % (4 + b)
+            mm(bank, T.wq[:, 128 * b:128 * b + 128], T.wsp[:, 128 * b:128 * b + 128], ["wq", "wsp"],
+               T.zq[:, :], T.zs[:, :], ["zq"])
+            if b in R_HOME:
+                ts(T.rb[:, b * C:(b + 1) * C], ["rb%d" % b, bank], T[bank][:, 0:C], [], 2.0 ** -6, A.mult, n=C)
+            else:
+                sg(T.rb[:, b * C:(b + 1) * C], ["rb%d" % b, bank], T[bank][:, 0:C], [], el(C), 2.0 ** -6)
+        for b in (2, 3):
+            sg(T.gp[:, b * C:(b + 1) * C], ["gp%d" % b], T.rb[:, b * C:(b + 1) * C].indirect(o), ["rb%d" % b, orr])
+        for b in (0, 1):
+            tt(T.xt[:, b:4 * C:4], ["xt%d" % b], T.rb[:, b * C:(b + 1) * C].indirect(o), T.fh[:, b * C:(b + 1) * C],
+               ["rb%d" % b, "fh%d" % b, orr], A.add, ga(C))
+        for b in (2, 3):
+            tt(T.xt[:, b:4 * C:4], ["xt%d" % b, "p%d" % b], T.gp[:, b * C:(b + 1) * C], T["p%d" % b][:, 0:C],
+               ["gp%d" % b], A.add, el(C))
+        quant(T["xq%d" % (r + 1)][:, :], T["xs%d" % (r + 1)][:, :], ["xt0", "xt1", "xt2", "xt3"], ["xq%d" % (r + 1)],
+              T.xt[:, :], 4 * C)
+        if not last:
+            send_codes(r + 1)
+        else:
+            sg(T.nlr[:, :], ["nlr"], T.jf[:, :].indirect(nfo[:, :]), ["jf", nfr])
+
+    quant(T.vq[:, :], T.vqs[:, :], ["vb"], ["vq"], T.vb[:, :], 512)
+    mm("p4", T.vq[:, :], T.vqs[:, :], ["vq"], T.xq3[:, :], T.xs3[:, :], ["xq3"])
+    sg(T.yb[:, :], ["yb", "p4"], T.p4[:, 0:C], [], el(C))
+
+    def store(out, in_, res, tail=2.0):
+        op("y", [res], [], lambda: g.sync.dma_start(out=out, in_=in_), 0.1, "lout", 16, tail)
+
+    store(T.nl[:, :], T.nlr[0:128:16, :], "nlr")
+    store(T.y[:, :], T.yb[:, :], "yb", 3.0)
+    store(T.oc[:, :], T.xq3[:, :].bitcast(dt.uint8), "xq3")
+    for k in range(4):
+        store(T.osc[4 * k:4 * k + 4, :], T.xs3[32 * k:32 * k + 4, :], "xq3")
+    emit()
+
+
+def relay_program(g, core, T, topo):
+    n = 0
+    for r in range(3):
+        for i, src in enumerate(T.cores):
+            dst = T.cores[i ^ MASKS[r]]
+            if relay_of(src, dst, topo) != core:
+                continue
+            g.wait_ge(T.sem["al%d" % r], NL)
+            n += send(g, T, topo, core, dst, T["lo%d" % r][:, :], T["lo%d" % r][:, :], "al%d" % r, NL)
+            g.wait_ge(T.sem["ac%d" % r], 2 * NE)
+            n += send(g, T, topo, core, dst, T["lc%d" % r][:, :].bitcast(dt.uint8),
+                      T["lc%d" % r][:, :].bitcast(dt.uint8), "ac%d" % r, NE)
+            n += send(g, T, topo, core, dst, T["ls%d" % r][:, :], T["ls%d" % r][:, :], "ac%d" % r, NE)
+    if n:
+        g.wait_ge(T.sem.sent, n)

@@ -3,16 +3,21 @@ from concourse.mybir import dt, AluOpType, ActivationFunctionType
 A = AluOpType
 COPY = ActivationFunctionType.Copy
 IDENT = ActivationFunctionType.Identity
+SIGN = ActivationFunctionType.Sign
 C = 288
 TC = C // 16
 MASKS = [4, 1, 2]
 LEVELS = [(3, 1), (3, 3), (2, 9), (2, 18), (2, 36), (2, 72), (2, 144)]
 PARTS = {"a": (0, 160), "b": (160, C)}
-Z_HOME = ()
+Z_HOME = (2,)
 TWIN_HOME = ()
-R_HOME = (0, 1)
+R_HOME = (1,)
 WAKE, GATHER, EL = 0.06, 1.5e-3, 1.04e-3
-LOOK, EDGE = 0.5, 0.3
+LOOK, EDGE = 1.0, 1.0
+HASTE = {"hr": -1.0, "er": -0.6, "sc": 0.6, "et": 0.3, "rb": 3.0, "fh": -0.6, "k": 0.3, "ho": -3.0, "gp": -3.0}
+AFTER = ["zq"]
+S_HOME = False
+P_FAR = (2, 3)
 NE, NL = 8, 2
 NMK = 6
 
@@ -36,7 +41,7 @@ _b("uq uk vq", 128, CODE)
 _b("uqs uks vqs", 128, "uint8")
 _b("et", 2048, "bfloat16")
 _b("ub vb", 512, "bfloat16")
-_b("fli mli ki ka k0 k1 k2 x1 o1", TC, "int32")
+_b("fli mli ki ka k0 k1 k2 x1", TC, "int32")
 _b("jf j16 key s s2 mc0 mc1 m0 m1 m2 y0 y1 y2 y3 za0 za1 zb0 zb1 mine mhi km ks yb nlr mbig", C, "float32")
 _b("jc mask keep frow srow cand", C, "bfloat16")
 _b("mk sc", NMK * C, "bfloat16")
@@ -44,9 +49,10 @@ _b("hr", 8 * C, "bfloat16")
 _b("er", 21 * C, "bfloat16")
 _b("ho", 7 * TC, "uint16")
 _b("uo", 8, "uint16")
-_b("c16 jt mtf lof hif ffc dfm dmt ta tb tb2 tc x2 x3 o2 o3", TC, "float32")
+_b("c16 jt mtf ffc ff dfm dmt ta tb tc x2 x3", TC, "float32")
 _b("pi p16i", 2, "int32")
-_b("pf p16", 2, "float32")
+_b("pn p16", 2, "float32")
+_b("diag", 256, "float32")
 _b("p0 p1 p2 p3 p4 p5 p6 p7", 512, "float32", "psum")
 
 SEMAPHORES = ["cv", "cs", "ct", "cp", "lx", "lu", "lv", "lf", "lm", "lw", "lq", "lout", "sent"]
@@ -82,6 +88,7 @@ def order(ops):
     for i in range(n - 1, -1, -1):
         o = ops[i]
         far[i] = o["c"] + o["tail"] + max([far[u] + WAKE for u in users[i]] or [0.0])
+    far = [far[i] + HASTE.get(ops[i]["kind"], 0.0) for i in range(n)]
     left = [len(o["deps"]) for o in ops]
     ready = [0.0] * n
     end = [0.0] * n
@@ -158,7 +165,7 @@ def rank_program(g, core, T, topo):
         for r in wr:
             acc[r] = [me, []]
         deps.discard(me)
-        ops.append(dict(q=qn, c=cost, tail=tail, deps=deps, fn=fn, sem=sem or own.get(qn), inc=inc, ev=ev, free=False))
+        ops.append(dict(q=qn, c=cost, tail=tail, kind=(wr or [""])[0].rstrip("0123456789"), deps=deps, fn=fn, sem=sem or own.get(qn), inc=inc, ev=ev, free=False))
         return me
 
     def emit():
@@ -306,11 +313,11 @@ def rank_program(g, core, T, topo):
     iota("c16", [[16, TC]], 0, TC)
     op("v", [], ["et"], lambda: V.memset(T.et[:, :], 0.0), 0.9)
     ts(T.p16i[:, :], ["p16i"], T.pi[:, :], ["pi"], 15, A.bitwise_and)
-    cp(T.pf[:, :], ["pf"], T.pi[:, :], ["pi"])
     cp(T.p16[:, :], ["p16"], T.p16i[:, :], ["p16i"])
-    ts(T.keep[:, :], ["keep"], T.j16[:, :], ["j16"], 1.0, A.min, n=C)
     ts(T.mask[:, :], ["mask"], T.j16[:, :], ["j16", "p16"], T.p16[:, 0:1], A.is_equal, n=C)
-    ts(T.jc[:, :], ["jc"], T.jf[:, :], ["jf"], float(-(C // 2)), A.add, n=C)
+    ts(T.pn[:, :], ["pn"], T.pi[:, :], ["pi"], -1.0, A.mult)
+    lin(T.jc[:, :], ["jc"], T.jf[:, :], ["jf"], 1.0, -(C // 2))
+    op("s", ["j16"], ["keep"], lambda: S.activation(T.keep[:, :], T.j16[:, :], SIGN), el(C))
     for k in (7, 15, 20):
         sg(eslot(k)[0], [eslot(k)[1]], T.jc[:, :], ["jc"], el(C))
     lin(T.mbig[:, :], ["mbig"], T.mask[:, :], ["mask"], 2e29, -1e29)
@@ -330,19 +337,19 @@ def rank_program(g, core, T, topo):
     cp(T.uo[:, :], ["uo"], T.c16[:, 0:8], ["c16"])
     cp(T.uk[:, :].bitcast(dt.uint32), ["uk"], T.uq[:, :].bitcast(dt.uint32).indirect(T.uo[:, :]), ["uq", "uo"], ga(128))
     cp(T.uks[:, :], ["uks"], T.uqs[:, :].indirect(T.uo[:, :]), ["uq", "uo"], ga(128))
+    op("s", ["jf", "pn"], ["d0"], lambda: S.activation(T.diag[:, 0:128], T.jf[:, 0:128], SIGN, bias=T.pn[:, 0:1]), el(128))
+    op("s", ["d0"], ["d1"], lambda: S.activation(T.diag[:, 128:256], T.diag[:, 0:128], ActivationFunctionType.Square), el(128))
     for b in range(4):
         lo = 512 * b
-        ts(T.et[:, lo + b:lo + 512:4], ["et%d" % b], T.jf[:, 0:128], ["jf", "pf", "et"], T.pf[:, 0:1], A.is_equal,
-           0.5, A.mult, n=128)
+        op("s", ["d1", "et"], ["et%d" % b], lambda lo=lo, b=b: S.activation(
+            T.et[:, lo + b:lo + 512:4], T.diag[:, 128:256], IDENT, bias=0.5, scale=-0.5), el(128))
     quant(T.eq[:, :], T.eqs[:, :], ["et", "et0", "et1", "et2", "et3"], ["eq"], T.et[:, :], 2048)
     cp(T.mo[:, :], ["mo"], T.mli[:, :], ["mli"])
     cp(T.mtf[:, :], ["mtf"], T.mli[:, :], ["mli"])
     ts(T.jt[:, :], ["jt"], T.c16[:, :], ["c16", "p16"], T.p16[:, 0:1], A.add)
-    tt(T.lof[:, :], ["lof"], T.mtf[:, :], T.jt[:, :], ["mtf", "jt"], A.min)
-    tt(T.hif[:, :], ["hif"], T.mtf[:, :], T.jt[:, :], ["mtf", "jt"], A.max)
+    tt(T.loo[:, :], ["loo"], T.mtf[:, :], T.jt[:, :], ["mtf", "jt"], A.min)
+    tt(T.hio[:, :], ["hio"], T.mtf[:, :], T.jt[:, :], ["mtf", "jt"], A.max)
     tt(T.dmt[:, :], ["dmt"], T.mtf[:, :], T.jt[:, :], ["mtf", "jt"], A.subtract)
-    cp(T.loo[:, :], ["loo"], T.lof[:, :], ["lof"])
-    cp(T.hio[:, :], ["hio"], T.hif[:, :], ["hif"])
 
     def hrow(k, frm, tab):
         w, wr = (T.jc[:, :], "jc") if frm is None else hslot(frm)
@@ -365,7 +372,10 @@ def rank_program(g, core, T, topo):
         mm("p4", T.uk[:, :], T.uks[:, :], ["uk", "uks"], xq[:, :], xs[:, :], xr)
         mm("p5", T.uk[:, :], T.uks[:, :], ["uk", "uks"], xq[:, :], xs[:, :], xr)
         sg(T.s[:, :], ["s", "p4"], T.p4[:, 0:C], [], el(C))
-        cp(T.s2[:, :], ["s2", "p5"], T.p5[:, 0:C], [], el(C))
+        if S_HOME:
+            cp(T.s2[:, :], ["s2", "p5"], T.p5[:, 0:C], [], el(C))
+        else:
+            sg(T.s2[:, :], ["s2", "p5"], T.p5[:, 0:C], [], el(C))
         for b in range(4):
             mm("p%d" % b, T.eq[:, 128 * b:128 * b + 128], T.eqs[:, 128 * b:128 * b + 128], ["eq"], xq[:, :], xs[:, :], xr)
         if r:
@@ -382,6 +392,7 @@ def rank_program(g, core, T, topo):
             sg(T.frow[:, :], ["frow"], T.jc[:, :].indirect(T.fo0[:, :]), ["jc", "fo0"])
             v, vr = conv(T.frow[:, :], ["frow"], T.mo[:, :], "mo")
             tt(T.dfm[:, :], ["dfm"], v, T.ffc[:, :], [vr, "ffc"], A.subtract)
+            cp(T.ff[:, :], ["ff"], T.fli[:, :], ["fli"])
         for k in range(6, -1, -1):
             erow(k, eo, eor)
         to_off(T.eo8[:, :], "eo8", *conv(eslot(0)[0], [eslot(0)[1]], eo, eor))
@@ -448,16 +459,13 @@ def rank_program(g, core, T, topo):
         ts(T.k1[:, :], ["k1"], T.ki[:, :], ["ki"], 3, A.logical_shift_right, 7, A.bitwise_and)
         ts(T.x1[:, :], ["x1"], T.k0[:, :], ["k0"], float(C), A.mult, float(C), A.add)
         ts(T.k2[:, :], ["k2"], T.ki[:, :], ["ki"], 6, A.logical_shift_right, 7, A.bitwise_and)
-        tt(T.o1[:, :], ["o1"], T.x1[:, :], T.ka[:, :], ["x1", "ka"], A.subtract)
+        tt(T.w1[:, :], ["w1"], T.x1[:, :], T.ka[:, :], ["x1", "ka"], A.subtract)
         ts(T.x2[:, :], ["x2"], T.k1[:, :], ["k1"], float(C), A.mult, float(C // 2), A.add)
         ts(T.x3[:, :], ["x3"], T.k2[:, :], ["k2"], float(C), A.mult, float(C // 2 - 3 * C), A.add)
-        cp(T.w1[:, :], ["w1"], T.o1[:, :], ["o1"])
         v, vr = conv(T.er[:, 0:8 * C], ["er%d" % k for k in range(8)], T.w1[:, :], "w1")
-        tt(T.o2[:, :], ["o2"], T.x2[:, :], v, ["x2", vr], A.add)
-        cp(T.w2[:, :], ["w2"], T.o2[:, :], ["o2"])
+        tt(T.w2[:, :], ["w2"], T.x2[:, :], v, ["x2", vr], A.add)
         v, vr = conv(T.er[:, 8 * C:16 * C], ["er%d" % k for k in range(8, 16)], T.w2[:, :], "w2")
-        tt(T.o3[:, :], ["o3"], T.x3[:, :], v, ["x3", vr], A.add)
-        cp(T.w3[:, :], ["w3"], T.o3[:, :], ["o3"])
+        tt(T.w3[:, :], ["w3"], T.x3[:, :], v, ["x3", vr], A.add)
         to_off(T.to[:, :], "to", *conv(T.er[:, 16 * C:21 * C], ["er%d" % k for k in range(16, 21)], T.w3[:, :], "w3"))
 
         for b in range(4):
@@ -471,21 +479,20 @@ def rank_program(g, core, T, topo):
         v, vr = scan(mk, mr, sc, sr)
         tt(T.ta[:, :], ["ta"], v, T.dfm[:, :], [vr, "dfm"], A.mult)
         tt(T.tb[:, :], ["tb"], v, T.dmt[:, :], [vr, "dmt"], A.mult)
-        tt(T.ffc[:, :], ["ffc"], T.ta[:, :], T.ffc[:, :], ["ta"], A.add)
-        to_off(nfo[:, :], nfr, T.ffc[:, :], "ffc")
+        tt(nfo[:, :], [nfr], T.ta[:, :], T.ff[:, :], ["ta", "ff"], A.add)
         if not last:
+            tt(T.ff[:, :], ["ff"], T.ta[:, :], T.ff[:, :], ["ta"], A.add)
             send_list(r + 1)
             ts(T.tc[:, :], ["tc"], T.ta[:, :], ["ta"], -2.0, A.mult)
             tt(T.dfm[:, :], ["dfm"], T.tc[:, :], T.dfm[:, :], ["tc"], A.add)
-        tt(T.tb2[:, :], ["tb2"], T.tb[:, :], T.jt[:, :], ["tb", "jt"], A.add)
-        cp(T.so[:, :], ["so"], T.tb2[:, :], ["tb2"])
+        tt(T.so[:, :], ["so"], T.tb[:, :], T.jt[:, :], ["tb", "jt"], A.add)
         sg(T.srow[:, :], ["srow"], T.jc[:, :].indirect(T.so[:, :]), ["jc", "so"])
         o, orr = htab(0)
-        to_off(o, orr, *conv(T.srow[:, :], ["srow"], o, orr))
         for b in range(4):
             tt(T.z[:, b:4 * C:4], ["z%d" % b], T.fh[:, b * C:(b + 1) * C].indirect(nfo[:, :]),
                T.gt[:, b * C:(b + 1) * C], ["fh%d" % b, "gt%d" % b, nfr], A.add, ga(C))
         quant(T.zq[:, :], T.zs[:, :], ["z0", "z1", "z2", "z3"], ["zq"], T.z[:, :], 4 * C)
+        to_off(o, orr, *conv(T.srow[:, :], ["srow"] + AFTER, o, orr))
         for b in (2, 3, 0, 1):
             bank = "p%d" % (4 + b)
             mm(bank, T.wq[:, 128 * b:128 * b + 128], T.wsp[:, 128 * b:128 * b + 128], ["wq", "wsp"],
@@ -494,12 +501,12 @@ def rank_program(g, core, T, topo):
                 ts(T.rb[:, b * C:(b + 1) * C], ["rb%d" % b, bank], T[bank][:, 0:C], [], 2.0 ** -6, A.mult, n=C)
             else:
                 sg(T.rb[:, b * C:(b + 1) * C], ["rb%d" % b, bank], T[bank][:, 0:C], [], el(C), 2.0 ** -6)
-        for b in (2, 3):
+        for b in P_FAR:
             sg(T.gp[:, b * C:(b + 1) * C], ["gp%d" % b], T.rb[:, b * C:(b + 1) * C].indirect(o), ["rb%d" % b, orr])
-        for b in (0, 1):
+        for b in [b for b in range(4) if b not in P_FAR]:
             tt(T.xt[:, b:4 * C:4], ["xt%d" % b], T.rb[:, b * C:(b + 1) * C].indirect(o), T.fh[:, b * C:(b + 1) * C],
                ["rb%d" % b, "fh%d" % b, orr], A.add, ga(C))
-        for b in (2, 3):
+        for b in P_FAR:
             tt(T.xt[:, b:4 * C:4], ["xt%d" % b, "p%d" % b], T.gp[:, b * C:(b + 1) * C], T["p%d" % b][:, 0:C],
                ["gp%d" % b], A.add, el(C))
         quant(T["xq%d" % (r + 1)][:, :], T["xs%d" % (r + 1)][:, :], ["xt0", "xt1", "xt2", "xt3"], ["xq%d" % (r + 1)],

from concourse.mybir import dt, AluOpType, ActivationFunctionType

A = AluOpType
COPY = ActivationFunctionType.Copy
IDENT = ActivationFunctionType.Identity
SIGN = ActivationFunctionType.Sign
C = 288
TC = C // 16
MASKS = [4, 1, 2]
LEVELS = [(3, 1), (3, 3), (2, 9), (2, 18), (2, 36), (2, 72), (2, 144)]
PARTS = {"a": (0, 160), "b": (160, C)}
Z_HOME = (2,)
TWIN_HOME = ()
R_HOME = (1,)
WAKE, GATHER, EL = 0.06, 1.5e-3, 1.04e-3
LOOK, EDGE = 1.0, 1.0
HASTE = {"hr": -1.0, "er": -0.6, "sc": 0.6, "et": 0.3, "rb": 3.0, "fh": -0.6, "k": 0.3, "ho": -3.0, "gp": -3.0}
AFTER = ["zq"]
S_HOME = False
P_FAR = (2, 3)
NE, NL = 8, 2
NMK = 6

SCRATCH = {}


def _b(names, n, dtype, where="sbuf"):
    for name in names.split():
        SCRATCH[name] = (where, [128, n], dtype)


CODE = "float8_e4m3fn_x4"
_b("x0 xt z fh fs gt", 4 * C, "bfloat16")
_b("rb gp", 4 * C, "float32")
_b("xq0 xq1 xq2 xq3 lc0 lc1 lc2 zq", C, CODE)
_b("xs0 xs1 xs2 xs3 ls0 ls1 ls2 zs", C, "uint8")
_b("fo0 fo1 fo2 fo3 lo0 lo1 lo2 w1 w2 w3 to mo loo hio eo8 eo64 so", TC, "uint16")
_b("wq eq", 512, CODE)
_b("wsp eqs", 512, "uint8")
_b("uq uk vq", 128, CODE)
_b("uqs uks vqs", 128, "uint8")
_b("et", 2048, "bfloat16")
_b("ub vb", 512, "bfloat16")
_b("fli mli ki ka k0 k1 k2 x1", TC, "int32")
_b("jf j16 key s s2 mc0 mc1 m0 m1 m2 y0 y1 y2 y3 za0 za1 zb0 zb1 mine mhi km ks yb nlr mbig", C, "float32")
_b("jc mask keep frow srow cand", C, "bfloat16")
_b("mk sc", NMK * C, "bfloat16")
_b("hr", 8 * C, "bfloat16")
_b("er", 21 * C, "bfloat16")
_b("ho", 7 * TC, "uint16")
_b("uo", 8, "uint16")
_b("c16 jt mtf ffc ff dfm dmt ta tb tc x2 x3", TC, "float32")
_b("pi p16i", 2, "int32")
_b("pn p16", 2, "float32")
_b("diag", 256, "float32")
_b("p0 p1 p2 p3 p4 p5 p6 p7", 512, "float32", "psum")

SEMAPHORES = ["cv", "cs", "ct", "cp", "lx", "lu", "lv", "lf", "lm", "lw", "lq", "lout", "sent"]
SEMAPHORES += ["ac%d" % r for r in range(3)] + ["al%d" % r for r in range(3)]


def relay_of(src, dst, topo):
    if topo.may_write(src, dst):
        return None
    cs = [c for c in topo.cores_of(src) if topo.may_write(c, dst)]
    near = [c for c in cs if topo.die(c) == topo.die(src)]
    return (near or cs)[0]


def send(g, T, topo, src, dst, out_ap, in_ap, sem, count):
    rid, pid = topo.addr(dst, src)
    e = topo.engines(src, dst)[:count]
    m = 0
    for k in e:
        m |= 1 << k
    g.remote_dma(out_ap=out_ap, in_ap=in_ap, remote_sem=T.sem[sem], local_sem=T.sem.sent, pid=pid, routing_id=rid,
                 dma_engine_mask=m)
    return len(e)


def order(ops):
    n = len(ops)
    users = [[] for _ in range(n)]
    for i, o in enumerate(ops):
        for d in o["deps"]:
            users[d].append(i)
    far = [0.0] * n
    for i in range(n - 1, -1, -1):
        o = ops[i]
        far[i] = o["c"] + o["tail"] + max([far[u] + WAKE for u in users[i]] or [0.0])
    far = [far[i] + HASTE.get(ops[i]["kind"], 0.0) for i in range(n)]
    left = [len(o["deps"]) for o in ops]
    ready = [0.0] * n
    end = [0.0] * n
    open_ = {}
    free = {}
    out = []

    def finish(i, t):
        end[i] = t
        for u in users[i]:
            left[u] -= 1
            ready[u] = max(ready[u], t if ops[i]["q"] == ops[u]["q"] and not ops[i]["tail"] and ops[i]["free"] else t + WAKE)
            if left[u] == 0:
                release(u)

    def release(u):
        if ops[u]["q"] is None:
            out.append(u)
            finish(u, ready[u] + ops[u]["tail"])
        else:
            open_.setdefault(ops[u]["q"], []).append(u)

    for i in range(n):
        if not ops[i]["deps"]:
            release(i)
    while any(open_.values()):
        pick = None
        for q, cand in open_.items():
            if not cand:
                continue
            t = max(free.get(q, 0.0), min(ready[i] for i in cand))
            now = [i for i in cand if ready[i] <= t + 1e-9]
            b = max(now, key=lambda i: (far[i], -i))
            stop = t + ops[b]["c"]
            for i in cand:
                if far[i] > far[b] + EDGE and ready[i] < stop and ready[i] - t < LOOK * (stop - ready[i]):
                    b = i
            s = max(t, ready[b])
            if pick is None or s < pick[0]:
                pick = (s, q, b)
        s, q, b = pick
        open_[q].remove(b)
        free[q] = s + ops[b]["c"]
        out.append(b)
        finish(b, free[q] + ops[b]["tail"])
    return out


def rank_program(g, core, T, topo):
    rank = T.rank_of(core)
    if rank is None:
        relay_program(g, core, T, topo)
        return
    queues = {"v": g.vector, "s": g.scalar, "t": g.tensor, "p": g, "y": g.sync}
    own = {"v": "cv", "s": "cs", "t": "ct", "p": "cp"}
    V, S, P = g.vector, g.scalar, g.tensor
    ops = []
    acc = {}

    def op(qn, rd, wr, fn, cost, sem=None, inc=1, tail=0.0, ev=None):
        deps = set()
        me = len(ops)
        for r in rd:
            a = acc.setdefault(r, [None, []])
            if a[0] is not None:
                deps.add(a[0])
        for r in wr:
            a = acc.setdefault(r, [None, []])
            deps.update(a[1])
            if a[0] is not None:
                deps.add(a[0])
        for r in rd:
            acc[r][1].append(me)
        for r in wr:
            acc[r] = [me, []]
        deps.discard(me)
        ops.append(dict(q=qn, c=cost, tail=tail, kind=(wr or [""])[0].rstrip("0123456789"), deps=deps, fn=fn, sem=sem or own.get(qn), inc=inc, ev=ev, free=False))
        return me

    def emit():
        total, know = {}, {k: {} for k in queues}
        for i in order(ops):
            o = ops[i]
            if o["q"] is None:
                o["knows"] = {}
                continue
            k = know[o["q"]]
            waits = sorted((ops[d]["ev"] + (d,) for d in o["deps"] if ops[d]["ev"]), key=lambda e: -len(ops[e[2]]["knows"]))
            top = {}
            for s, n, d in waits:
                if n > top.get(s, (0,))[0]:
                    top[s] = (n, d)
            for s, n, d in waits:
                if top[s] != (n, d) or k.get(s, 0) >= n:
                    continue
                queues[o["q"]].wait_ge(T.sem[s], n)
                for a, b in ops[d]["knows"].items():
                    if k.get(a, 0) < b:
                        k[a] = b
                k[s] = n
            if o["sem"] is None:
                o["fn"]()
                o["knows"] = {}
                continue
            total[o["sem"]] = total.get(o["sem"], 0) + o["inc"]
            o["fn"]().then_inc(T.sem[o["sem"]], o["inc"])
            o["ev"] = (o["sem"], total[o["sem"]])
            o["knows"] = dict(k)
            o["knows"][o["sem"]] = total[o["sem"]]
        for s in sorted(total):
            if know["p"].get(s, 0) < total[s]:
                g.wait_ge(T.sem[s], total[s])
        g.wait_ge(T.sem.sent, sends[0])

    def el(n, k=1.0):
        return max(n * k, 64) * EL

    def ga(n):
        return 0.055 + n * GATHER

    def ts(out, ow, in0, ir, s1, o1, s2=None, o2=None, n=TC):
        if o2 is None:
            op("v", ir, ow, lambda: V.tensor_scalar(out, in0, s1, None, o1), el(n))
        else:
            op("v", ir, ow, lambda: V.tensor_scalar(out, in0, s1, s2, o1, o2), el(n))

    def tt(out, ow, a, b, ir, o, c=None):
        op("v", ir, ow, lambda: V.tensor_tensor(out, a, b, o), el(TC) if c is None else c)

    def cp(out, ow, a, ir, c=None):
        op("v", ir, ow, lambda: V.tensor_copy(out, a), el(TC) if c is None else c)

    def sg(out, ow, a, ir, c=None, scale=None):
        c = ga(C) if c is None else c
        if scale is None:
            op("s", ir, ow, lambda: S.activation(out, a, COPY), c)
        else:
            op("s", ir, ow, lambda: S.activation(out, a, COPY, scale=scale), c)

    def lin(out, ow, a, ir, scale, bias, n=C):
        op("s", ir, ow, lambda: S.activation(out, a, IDENT, bias=float(bias), scale=float(scale)), el(n))

    def hslot(k):
        return T.hr[:, k * C:(k + 1) * C], "hr%d" % k

    def eslot(k):
        return T.er[:, k * C:(k + 1) * C], "er%d" % k

    def htab(k):
        return T.ho[:, k * TC:(k + 1) * TC], "ho%d" % k

    rot = [0]

    def turn_mk():
        k = rot[0] % NMK
        rot[0] += 1
        return T.mk[:, k * C:(k + 1) * C], "mk%d" % k, k, "sc%d" % k

    def scan(mk, mr, k, sr):
        op("v", [mr, "keep"], [sr],
           lambda: V.tensor_tensor_scan(T.sc[:, k * C:(k + 1) * C], T.keep[:, :], mk, 0.0, A.mult, A.add), el(C, 0.5))
        return T.sc[:, k * C + 15:(k + 1) * C:16], sr

    def conv(win, wr, off, orr):
        mk, mr, sc, sr = turn_mk()
        tt(mk, [mr], win.indirect(off), T.mask[:, :], wr + [orr, "mask"], A.mult, ga(C))
        return scan(mk, mr, sc, sr)

    def to_off(out, ow, view, vr):
        ts(out, [ow], view, [vr], float(C // 2), A.add)

    def mm(bank, st, sts, sr, mv, mvs, mr):
        op("t", sr + mr, [bank], lambda: P.matmul_mx(T[bank][:, 0:C], st, sts, mv, mvs, True, True), 0.3)

    def quant(q, s, rd, wr, src, n):
        op("v", rd, wr, lambda: V.quantize_mx(q, s, src), 0.012 + 0.28e-3 * n)

    def load(qn, out, in_, res, sem, tail=2.0):
        op(qn, [], [res], lambda: queues[qn].dma_start(out=out, in_=in_), 0.1, sem, 16, tail)

    sends = [0]

    def to_partner(r, bufs, sem, count, n, land, tail):
        dst = T.cores[rank ^ MASKS[r]]
        via = relay_of(core, dst, topo)
        hop = dst if via is None else via
        ids = []

        def go(o, i):
            sends[0] += send(g, T, topo, core, hop, o, i, sem, count)

        for o, i, res in bufs:
            op("p", [res], ["out" + sem], lambda o=o, i=i: go(o, i), 0.5)
            ops[-1]["sem"] = None
        op(None, ["out" + sem], [land], None, 0.0, None, 0, tail if via is None else 2 * tail, (sem, n))

    def send_list(r):
        to_partner(r, [(T["lo%d" % r][:, :], T["fo%d" % r][:, :], "fo%d" % r)], "al%d" % r, NL, NL, "lo%d" % r, 4.0)

    def send_codes(r):
        to_partner(r, [(T["lc%d" % r][:, :].bitcast(dt.uint8), T["xq%d" % r][:, :].bitcast(dt.uint8), "xq%d" % r),
                       (T["ls%d" % r][:, :], T["xs%d" % r][:, :], "xq%d" % r)], "ac%d" % r, NE, 2 * NE, "lc%d" % r, 7.0)

    load("y", T.fli[:, :], T.fl[:, :], "fli", "lf")
    load("s", T.x0[:, :], T.x[:, :], "x0", "lx", 3.0)
    load("y", T.ub[:, :], T.u[:, :], "ub", "lu")
    load("y", T.mli[:, :], T.ml[:, :], "mli", "lm")
    load("y", T.wq[:, :].bitcast(dt.uint8), T.wc[:, :], "wq", "lw")
    load("y", T.wsp[:, :], T.ws[:, :], "wsp", "lq")
    load("y", T.vb[:, :], T.v[:, :], "vb", "lv")

    def iota(name, pattern, mult, n, flag=True):
        if flag:
            op("p", [], [name], lambda: g.iota(T[name][:, :], pattern, 0, mult, allow_small_or_imprecise_dtypes=True),
               0.13 + 2 * n * EL)
        else:
            op("p", [], [name], lambda: g.iota(T[name][:, :], pattern, 0, mult), 0.13 + 2 * n * EL)

    iota("pi", [[0, 2]], 1, 2, False)
    iota("j16", [[0, TC], [1, 16]], 0, C)
    iota("jf", [[1, C]], 0, C)
    iota("c16", [[16, TC]], 0, TC)
    op("v", [], ["et"], lambda: V.memset(T.et[:, :], 0.0), 0.9)
    ts(T.p16i[:, :], ["p16i"], T.pi[:, :], ["pi"], 15, A.bitwise_and)
    cp(T.p16[:, :], ["p16"], T.p16i[:, :], ["p16i"])
    ts(T.mask[:, :], ["mask"], T.j16[:, :], ["j16", "p16"], T.p16[:, 0:1], A.is_equal, n=C)
    ts(T.pn[:, :], ["pn"], T.pi[:, :], ["pi"], -1.0, A.mult)
    lin(T.jc[:, :], ["jc"], T.jf[:, :], ["jf"], 1.0, -(C // 2))
    op("s", ["j16"], ["keep"], lambda: S.activation(T.keep[:, :], T.j16[:, :], SIGN), el(C))
    for k in (7, 15, 20):
        sg(eslot(k)[0], [eslot(k)[1]], T.jc[:, :], ["jc"], el(C))
    lin(T.mbig[:, :], ["mbig"], T.mask[:, :], ["mask"], 2e29, -1e29)
    lin(T.key[:, :], ["key"], T.jf[:, :], ["jf"], -512.0, 512 * C + 224)

    cp(T.fo0[:, :], ["fo0"], T.fli[:, :], ["fli"])
    send_list(0)
    op("v", ["jc", "fo0"], ["hr0"], lambda: V.tensor_copy(T.hr[:, 0:C].indirect(T.fo0[:, :]), T.jc[:, :]), 1.0)
    mk, mr, sc, sr = turn_mk()
    tt(mk, [mr], T.hr[:, 0:C], T.mask[:, :], ["hr0", "mask"], A.mult, el(C, 2))
    to_off(htab(0)[0], "ho0", *scan(mk, mr, sc, sr))
    ts(T.ffc[:, :], ["ffc"], T.fli[:, :], ["fli"], float(-(C // 2)), A.add)

    quant(T.xq0[:, :], T.xs0[:, :], ["x0"], ["xq0"], T.x0[:, :], 4 * C)
    send_codes(0)
    quant(T.uq[:, :], T.uqs[:, :], ["ub"], ["uq"], T.ub[:, :], 512)
    cp(T.uo[:, :], ["uo"], T.c16[:, 0:8], ["c16"])
    cp(T.uk[:, :].bitcast(dt.uint32), ["uk"], T.uq[:, :].bitcast(dt.uint32).indirect(T.uo[:, :]), ["uq", "uo"], ga(128))
    cp(T.uks[:, :], ["uks"], T.uqs[:, :].indirect(T.uo[:, :]), ["uq", "uo"], ga(128))
    op("s", ["jf", "pn"], ["d0"], lambda: S.activation(T.diag[:, 0:128], T.jf[:, 0:128], SIGN, bias=T.pn[:, 0:1]), el(128))
    op("s", ["d0"], ["d1"], lambda: S.activation(T.diag[:, 128:256], T.diag[:, 0:128], ActivationFunctionType.Square), el(128))
    for b in range(4):
        lo = 512 * b
        op("s", ["d1", "et"], ["et%d" % b], lambda lo=lo, b=b: S.activation(
            T.et[:, lo + b:lo + 512:4], T.diag[:, 128:256], IDENT, bias=0.5, scale=-0.5), el(128))
    quant(T.eq[:, :], T.eqs[:, :], ["et", "et0", "et1", "et2", "et3"], ["eq"], T.et[:, :], 2048)
    cp(T.mo[:, :], ["mo"], T.mli[:, :], ["mli"])
    cp(T.mtf[:, :], ["mtf"], T.mli[:, :], ["mli"])
    ts(T.jt[:, :], ["jt"], T.c16[:, :], ["c16", "p16"], T.p16[:, 0:1], A.add)
    tt(T.loo[:, :], ["loo"], T.mtf[:, :], T.jt[:, :], ["mtf", "jt"], A.min)
    tt(T.hio[:, :], ["hio"], T.mtf[:, :], T.jt[:, :], ["mtf", "jt"], A.max)
    tt(T.dmt[:, :], ["dmt"], T.mtf[:, :], T.jt[:, :], ["mtf", "jt"], A.subtract)

    def hrow(k, frm, tab):
        w, wr = (T.jc[:, :], "jc") if frm is None else hslot(frm)
        o, orr = htab(tab)
        sg(hslot(k)[0], [hslot(k)[1]], w.indirect(o), [wr, orr])

    def hconv(frm, tab, new):
        w, wr = hslot(frm)
        o, orr = htab(tab)
        to_off(*htab(new), *conv(w, [wr], o, orr))

    def erow(k, off, orr):
        w, wr = eslot(k + 1)
        sg(eslot(k)[0], [eslot(k)[1]], w.indirect(off), [wr, orr])

    for r in range(3):
        last = r == 2
        xq, xs, xr = T["xq%d" % r], T["xs%d" % r], ["xq%d" % r]
        eo, eor = T["lo%d" % r][:, :], "lo%d" % r
        mm("p4", T.uk[:, :], T.uks[:, :], ["uk", "uks"], xq[:, :], xs[:, :], xr)
        mm("p5", T.uk[:, :], T.uks[:, :], ["uk", "uks"], xq[:, :], xs[:, :], xr)
        sg(T.s[:, :], ["s", "p4"], T.p4[:, 0:C], [], el(C))
        if S_HOME:
            cp(T.s2[:, :], ["s2", "p5"], T.p5[:, 0:C], [], el(C))
        else:
            sg(T.s2[:, :], ["s2", "p5"], T.p5[:, 0:C], [], el(C))
        for b in range(4):
            mm("p%d" % b, T.eq[:, 128 * b:128 * b + 128], T.eqs[:, 128 * b:128 * b + 128], ["eq"], xq[:, :], xs[:, :], xr)
        if r:
            hrow(0, None, 0)
        hrow(1, 0, 0)
        hrow(2, 1, 0)
        hconv(1, 0, 1)
        hrow(3, 2, 1)
        for k in range(5):
            hconv(3 + k, 1 + k, 2 + k)
            if k < 4:
                hrow(4 + k, 3 + k, 1 + k)
        if r == 0:
            sg(T.frow[:, :], ["frow"], T.jc[:, :].indirect(T.fo0[:, :]), ["jc", "fo0"])
            v, vr = conv(T.frow[:, :], ["frow"], T.mo[:, :], "mo")
            tt(T.dfm[:, :], ["dfm"], v, T.ffc[:, :], [vr, "ffc"], A.subtract)
            cp(T.ff[:, :], ["ff"], T.fli[:, :], ["fli"])
        for k in range(6, -1, -1):
            erow(k, eo, eor)
        to_off(T.eo8[:, :], "eo8", *conv(eslot(0)[0], [eslot(0)[1]], eo, eor))
        for k in range(14, 7, -1):
            erow(k, T.eo8[:, :], "eo8")
        to_off(T.eo64[:, :], "eo64", *conv(eslot(8)[0], [eslot(8)[1]], T.eo8[:, :], "eo8"))
        for k in range(19, 15, -1):
            erow(k, T.eo64[:, :], "eo64")

        cur = "s"
        turn = 0
        for level, (rad, n) in enumerate(LEVELS):
            o, orr = htab(level)
            base, side = cur, "s2"
            if level:
                side = "mc%d" % (level % 2)
                if level in TWIN_HOME:
                    cp(T[side][:, :], [side], T[cur][:, :], [cur], el(C))
                else:
                    sg(T[side][:, :], [side], T[cur][:, :], [cur], el(C))
            for i in range(rad - 1):
                d = "m%d" % (turn % 3)
                turn += 1
                z = base if i else side
                tt(T[d][:, :], [d], T[cur][:, :].indirect(o), T[z][:, :], [cur, z, orr], A.max, ga(C))
                cur = d
        tt(T.cand[:, :], ["cand", "p5"], T[cur][:, :], T.p5[:, 0:C], [cur], A.is_equal, el(C))
        for p, (lo, hi) in PARTS.items():
            tt(T.y0[:, lo:hi], ["y0" + p], T.cand[:, lo:hi], T.key[:, lo:hi], ["cand", "key"], A.mult, el(hi - lo, 2))
        cur = "y0"
        turn = 1
        for level, (rad, n) in enumerate(LEVELS):
            orr = htab(level)[1]
            base = cur
            for i in range(rad - 1):
                zz = "z%s%d" % ("ab"[i], level % 2)
                for p, (lo, hi) in PARTS.items():
                    if level in Z_HOME:
                        ts(T[zz][:, lo:hi], [zz + p], T[base][:, lo:hi], [base + p], float(n * (i + 1)), A.add, n=hi - lo)
                    else:
                        lin(T[zz][:, lo:hi], [zz + p], T[base][:, lo:hi], [base + p], 1.0, n * (i + 1), hi - lo)
            for i in range(rad - 1):
                zz = "z%s%d" % ("ab"[i], level % 2)
                d = "y%d" % (turn % 4)
                turn += 1
                for p, (lo, hi) in PARTS.items():
                    off = T.ho[:, level * TC + lo // 16:level * TC + hi // 16]
                    tt(T[d][:, lo:hi], [d + p], T[cur][:, :].indirect(off), T[zz][:, lo:hi],
                       [cur + q for q in PARTS] + [zz + p, orr], A.max, ga(hi - lo))
                cur = d
        for b in range(4):
            sg(T.fh[:, b * C:(b + 1) * C], ["fh%d" % b, "p%d" % b], T["p%d" % b][:, 0:C], [], el(C))
        for b in range(4):
            mm("p%d" % (4 + b), T.eq[:, 128 * b:128 * b + 128], T.eqs[:, 128 * b:128 * b + 128], ["eq"],
               T["lc%d" % r][:, :], T["ls%d" % r][:, :], ["lc%d" % r])
            sg(T.fs[:, b * C:(b + 1) * C], ["fs%d" % b, "p%d" % (4 + b)], T["p%d" % (4 + b)][:, 0:C], [], el(C))

        tt(T.km[:, :], ["km"], T[cur][:, :], T.mask[:, :], [cur + p for p in PARTS] + ["mask"], A.mult, el(C, 2))
        op("v", ["km", "keep"], ["ks"],
           lambda: V.tensor_tensor_scan(T.ks[:, :], T.keep[:, :], T.km[:, :], 0.0, A.mult, A.add), el(C))
        cp(T.ki[:, :], ["ki"], T.ks[:, 15:C:16], ["ks"])
        ts(T.k0[:, :], ["k0"], T.ki[:, :], ["ki"], 7, A.bitwise_and)
        ts(T.ka[:, :], ["ka"], T.ki[:, :], ["ki"], 9, A.logical_shift_right)
        ts(T.k1[:, :], ["k1"], T.ki[:, :], ["ki"], 3, A.logical_shift_right, 7, A.bitwise_and)
        ts(T.x1[:, :], ["x1"], T.k0[:, :], ["k0"], float(C), A.mult, float(C), A.add)
        ts(T.k2[:, :], ["k2"], T.ki[:, :], ["ki"], 6, A.logical_shift_right, 7, A.bitwise_and)
        tt(T.w1[:, :], ["w1"], T.x1[:, :], T.ka[:, :], ["x1", "ka"], A.subtract)
        ts(T.x2[:, :], ["x2"], T.k1[:, :], ["k1"], float(C), A.mult, float(C // 2), A.add)
        ts(T.x3[:, :], ["x3"], T.k2[:, :], ["k2"], float(C), A.mult, float(C // 2 - 3 * C), A.add)
        v, vr = conv(T.er[:, 0:8 * C], ["er%d" % k for k in range(8)], T.w1[:, :], "w1")
        tt(T.w2[:, :], ["w2"], T.x2[:, :], v, ["x2", vr], A.add)
        v, vr = conv(T.er[:, 8 * C:16 * C], ["er%d" % k for k in range(8, 16)], T.w2[:, :], "w2")
        tt(T.w3[:, :], ["w3"], T.x3[:, :], v, ["x3", vr], A.add)
        to_off(T.to[:, :], "to", *conv(T.er[:, 16 * C:21 * C], ["er%d" % k for k in range(16, 21)], T.w3[:, :], "w3"))

        for b in range(4):
            sg(T.gt[:, b * C:(b + 1) * C], ["gt%d" % b], T.fs[:, b * C:(b + 1) * C].indirect(T.to[:, :]),
               ["fs%d" % b, "to"])
        nfo, nfr = T["fo%d" % (r + 1)], "fo%d" % (r + 1)
        cp(T.mine[:, :], ["mine"], T.s[:, :].indirect(T.to[:, :]), ["s", "to"], ga(C))
        tt(T.mhi[:, :], ["mhi"], T.mine[:, :].indirect(T.hio[:, :]), T.mbig[:, :], ["mine", "hio", "mbig"], A.min, ga(C))
        mk, mr, sc, sr = turn_mk()
        tt(mk, [mr], T.mine[:, :].indirect(T.loo[:, :]), T.mhi[:, :], ["mine", "mhi", "loo"], A.is_lt, ga(C))
        v, vr = scan(mk, mr, sc, sr)
        tt(T.ta[:, :], ["ta"], v, T.dfm[:, :], [vr, "dfm"], A.mult)
        tt(T.tb[:, :], ["tb"], v, T.dmt[:, :], [vr, "dmt"], A.mult)
        tt(nfo[:, :], [nfr], T.ta[:, :], T.ff[:, :], ["ta", "ff"], A.add)
        if not last:
            tt(T.ff[:, :], ["ff"], T.ta[:, :], T.ff[:, :], ["ta"], A.add)
            send_list(r + 1)
            ts(T.tc[:, :], ["tc"], T.ta[:, :], ["ta"], -2.0, A.mult)
            tt(T.dfm[:, :], ["dfm"], T.tc[:, :], T.dfm[:, :], ["tc"], A.add)
        tt(T.so[:, :], ["so"], T.tb[:, :], T.jt[:, :], ["tb", "jt"], A.add)
        sg(T.srow[:, :], ["srow"], T.jc[:, :].indirect(T.so[:, :]), ["jc", "so"])
        o, orr = htab(0)
        for b in range(4):
            tt(T.z[:, b:4 * C:4], ["z%d" % b], T.fh[:, b * C:(b + 1) * C].indirect(nfo[:, :]),
               T.gt[:, b * C:(b + 1) * C], ["fh%d" % b, "gt%d" % b, nfr], A.add, ga(C))
        quant(T.zq[:, :], T.zs[:, :], ["z0", "z1", "z2", "z3"], ["zq"], T.z[:, :], 4 * C)
        to_off(o, orr, *conv(T.srow[:, :], ["srow"] + AFTER, o, orr))
        for b in (2, 3, 0, 1):
            bank = "p%d" % (4 + b)
            mm(bank, T.wq[:, 128 * b:128 * b + 128], T.wsp[:, 128 * b:128 * b + 128], ["wq", "wsp"],
               T.zq[:, :], T.zs[:, :], ["zq"])
            if b in R_HOME:
                ts(T.rb[:, b * C:(b + 1) * C], ["rb%d" % b, bank], T[bank][:, 0:C], [], 2.0 ** -6, A.mult, n=C)
            else:
                sg(T.rb[:, b * C:(b + 1) * C], ["rb%d" % b, bank], T[bank][:, 0:C], [], el(C), 2.0 ** -6)
        for b in P_FAR:
            sg(T.gp[:, b * C:(b + 1) * C], ["gp%d" % b], T.rb[:, b * C:(b + 1) * C].indirect(o), ["rb%d" % b, orr])
        for b in [b for b in range(4) if b not in P_FAR]:
            tt(T.xt[:, b:4 * C:4], ["xt%d" % b], T.rb[:, b * C:(b + 1) * C].indirect(o), T.fh[:, b * C:(b + 1) * C],
               ["rb%d" % b, "fh%d" % b, orr], A.add, ga(C))
        for b in P_FAR:
            tt(T.xt[:, b:4 * C:4], ["xt%d" % b, "p%d" % b], T.gp[:, b * C:(b + 1) * C], T["p%d" % b][:, 0:C],
               ["gp%d" % b], A.add, el(C))
        quant(T["xq%d" % (r + 1)][:, :], T["xs%d" % (r + 1)][:, :], ["xt0", "xt1", "xt2", "xt3"], ["xq%d" % (r + 1)],
              T.xt[:, :], 4 * C)
        if not last:
            send_codes(r + 1)
        else:
            sg(T.nlr[:, :], ["nlr"], T.jf[:, :].indirect(nfo[:, :]), ["jf", nfr])

    quant(T.vq[:, :], T.vqs[:, :], ["vb"], ["vq"], T.vb[:, :], 512)
    mm("p4", T.vq[:, :], T.vqs[:, :], ["vq"], T.xq3[:, :], T.xs3[:, :], ["xq3"])
    sg(T.yb[:, :], ["yb", "p4"], T.p4[:, 0:C], [], el(C))

    def store(out, in_, res, tail=2.0):
        op("y", [res], [], lambda: g.sync.dma_start(out=out, in_=in_), 0.1, "lout", 16, tail)

    store(T.nl[:, :], T.nlr[0:128:16, :], "nlr")
    store(T.y[:, :], T.yb[:, :], "yb", 3.0)
    store(T.oc[:, :], T.xq3[:, :].bitcast(dt.uint8), "xq3")
    for k in range(4):
        store(T.osc[4 * k:4 * k + 4, :], T.xs3[32 * k:32 * k + 4, :], "xq3")
    emit()


def relay_program(g, core, T, topo):
    n = 0
    for r in range(3):
        for i, src in enumerate(T.cores):
            dst = T.cores[i ^ MASKS[r]]
            if relay_of(src, dst, topo) != core:
                continue
            g.wait_ge(T.sem["al%d" % r], NL)
            n += send(g, T, topo, core, dst, T["lo%d" % r][:, :], T["lo%d" % r][:, :], "al%d" % r, NL)
            g.wait_ge(T.sem["ac%d" % r], 2 * NE)
            n += send(g, T, topo, core, dst, T["lc%d" % r][:, :].bitcast(dt.uint8),
                      T["lc%d" % r][:, :].bitcast(dt.uint8), "ac%d" % r, NE)
            n += send(g, T, topo, core, dst, T["ls%d" % r][:, :], T["ls%d" % r][:, :], "ac%d" % r, NE)
    if n:
        g.wait_ge(T.sem.sent, n)
